import numpy as np
import ml_dtypes


def mxq(x, axis, fmt="e4m3"):
    dtype, down = {"e4m3": (ml_dtypes.float8_e4m3fn, 7), "e5m2": (ml_dtypes.float8_e5m2, 14)}[fmt]
    v = np.moveaxis(np.asarray(x, np.float32).astype(ml_dtypes.bfloat16).astype(np.float64), axis, -1)
    blocks = v.reshape(v.shape[:-1] + (-1, 32))
    amax = np.abs(blocks).max(-1, keepdims=True)
    byte = np.maximum(np.where(amax > 0, np.frexp(amax)[1] - 1 + 127, 0) - down, 1)
    scale = np.exp2(byte - 127.0)
    codes = (blocks / scale).astype(np.float32).astype(dtype).astype(np.float64)
    return np.moveaxis((codes * scale).reshape(v.shape), -1, axis)


WIDE = False


def mx_kscale(k):
    if not WIDE:
        return np.ones(k)
    levels = np.array([10, -10, 5, -5, 0])
    if k % 512:
        return np.exp2(np.random.permutation(np.resize(levels, k // 32))).repeat(32)
    a = np.empty((k // 512, 16))
    for p in range(k // 512):
        a[p, :8] = np.random.permutation(np.resize(levels, 8))
        for g in range(8):
            far = levels[np.abs(levels - a[p, g]) >= 10]
            a[p, g + 8] = far[np.random.randint(len(far))]
    return np.exp2(a.ravel()).repeat(32)


def f64(x):
    return np.asarray(x).astype(np.float64)


def striped(idx):
    return np.tile(idx.reshape(-1, 16).T, (8, 1)).astype(np.uint16)


def unstriped(offs):
    return offs[:16].T.reshape(-1).astype(np.int64)


E2M1 = np.array([0.0, 0.5, 1.0, 1.5, 2.0, 3.0, 4.0, 6.0, -0.0, -0.5, -1.0, -1.5, -2.0, -3.0, -4.0, -6.0])


def pack_weight(w, fmt):
    k, n = w.shape
    w = f64(np.asarray(w, np.float32).astype(ml_dtypes.bfloat16)).reshape(k // 32, 32, n)
    amax = np.abs(w).max(1)
    if fmt == "e4m3":
        byte = np.frexp(amax)[1] - 1 + 127 - 7
    else:
        mant, ex = np.frexp(amax / 6.0)
        byte = np.where(mant > 0.5, ex, ex - 1) + 127
    byte = np.clip(np.where(amax > 0, byte, 1), 1, 254)
    scaled = (w * np.exp2(127.0 - byte)[:, None, :]).reshape(k, n).astype(np.float32)
    by_word = np.ascontiguousarray(scaled.reshape(k // 512, 128, 4, n).transpose(0, 1, 3, 2))
    if fmt == "e4m3":
        words = by_word.astype(ml_dtypes.float8_e4m3fn).view(np.uint8)
    else:
        c = by_word.astype(ml_dtypes.float4_e2m1fn).view(np.uint8) & 0xF
        words = (c[..., 0::2] | (c[..., 1::2] << 4)).reshape(k // 512, 128, 2 * n)
    return np.ascontiguousarray(words), np.ascontiguousarray(byte.astype(np.uint8).reshape(k // 512, 16, n))


def unpack_weight(words, scales, fmt):
    g, _, n = scales.shape
    words = np.ascontiguousarray(words).reshape(g, 128, n, -1)
    if fmt == "e4m3":
        vals = words.view(ml_dtypes.float8_e4m3fn).astype(np.float64)
    else:
        nib = np.empty((g, 128, n, 4), np.uint8)
        nib[..., 0::2] = words & 0xF
        nib[..., 1::2] = words >> 4
        vals = E2M1[nib]
    vals = vals * np.repeat(np.exp2(scales.astype(np.float64) - 127.0), 8, axis=1)[..., None]
    return vals.transpose(0, 1, 3, 2).reshape(g * 512, n)


def gelu(v):
    return 0.5 * v * (1.0 + np.tanh(np.sqrt(2.0 / np.pi) * (v + 0.044715 * v**3)))


K, H, N, K2, T, S, T3, P = 1024, 1024, 512, 512, 4096, 1024, 2048, 512

def setup_inputs():
    n = np.random.standard_normal
    s = mx_kscale(K)[:, None]
    s2 = mx_kscale(K2)[:, None]
    u = mx_kscale(H)[:, None]
    tab_words, tab_scales = pack_weight(n((K, T)) * s, "e4m3")
    tab2_words, tab2_scales = pack_weight(n((K2, T3)) * s2, "e4m3")
    w2_words, w2_scales = pack_weight(1.3 * n((H, N)) / np.sqrt(H) / u, "e2m1")
    wb_words, wb_scales = pack_weight(n((K2, N)) / np.sqrt(K2) / s2, "e4m3")
    return {
        "tab_words": tab_words, "tab_scales": tab_scales,
        "tab2_words": tab2_words, "tab2_scales": tab2_scales,
        "offs": striped(np.random.permutation(T)[:S]),
        "offs2": striped(np.random.permutation(T3)[:P]),
        "pos1": striped(np.random.permutation(S)[:P]),
        "w1": (1.3 * n((K, H)) / np.sqrt(K) / s).astype(np.float32),
        "b1": (0.7 * n(H)).astype(np.float32),
        "gain": (np.exp(0.3 * n(H)) * u[:, 0]).astype(np.float32),
        "w2_words": w2_words, "w2_scales": w2_scales,
        "wa": (n((K2, N)) / np.sqrt(K2) / s2).astype(np.float32),
        "ba": (0.7 * n(N)).astype(np.float32),
        "wb_words": wb_words, "wb_scales": wb_scales,
    }

def reference(tab_words, tab_scales, tab2_words, tab2_scales, offs, offs2, pos1,
              w1, b1, gain, w2_words, w2_scales, wa, ba, wb_words, wb_scales):
    v = unpack_weight(tab_words, tab_scales, "e4m3")[:, unstriped(offs)]
    v2 = unpack_weight(tab2_words, tab2_scales, "e4m3")[:, unstriped(offs2)]
    w2 = unpack_weight(w2_words, w2_scales, "e2m1")
    wb = unpack_weight(wb_words, wb_scales, "e4m3")
    tr = mxq(f64(w1), 0, "e4m3").T @ v
    h = f64(gain)[:, None] * np.tanh(tr + f64(b1)[:, None])
    y = w2.T @ mxq(h, 0, "e4m3")
    qa = mxq(f64(wa), 0, "e4m3").T @ v2
    qb = wb.T @ v2
    top = np.maximum(qa + f64(ba)[:, None], qb)
    return y[:, unstriped(pos1)] + top

@@ -1,0 +1,280 @@
+from contextlib import ExitStack
+
+import concourse.mybir as mybir
+from concourse.masks import make_identity
+
+K, H, N, K2, T, S, T3, PICKS = 1024, 1024, 512, 512, 4096, 1024, 2048, 512
+FLOPS = 2 * K * H * S + 2 * H * N * S + 2 * 2 * K2 * N * PICKS
+
+F32 = mybir.dt.float32
+BF16 = mybir.dt.bfloat16
+I32 = mybir.dt.int32
+U32 = mybir.dt.uint32
+U16 = mybir.dt.uint16
+U8 = mybir.dt.uint8
+FP8X4 = mybir.dt.float8_e4m3fn_x4
+FP4X4 = mybir.dt.float4_e2m1fn_x4
+ACT = mybir.ActivationFunctionType
+ALU = mybir.AluOpType
+
+P = 128
+PACK = 4
+K_PASS = P * PACK
+BANK = 512
+QUADS = 4
+
+
+def tile_list_inhaler_technique_grading_kernel(
+    tc, tab_words, tab_scales, tab2_words, tab2_scales, offs, offs2, pos1,
+    w1, b1, gain, w2_words, w2_scales, wa, ba, wb_words, wb_scales, out,
+):
+    nc = tc.nc
+    with ExitStack() as ctx:
+        sb = ctx.enter_context(tc.tile_pool(name="sb", bufs=1))
+        reuse = ctx.enter_context(tc.tile_pool(name="reuse", bufs=1))
+        psum = ctx.enter_context(tc.psum_pool(name="psum", bufs=1))
+
+        def tile(name, shape, dtype):
+            return sb.tile(shape, dtype, name=name, align_bytes=64)
+
+        def placed(name, shape, dtype, kib):
+            return reuse.tile(shape, dtype, name=name, align_bytes=64, offset=kib * 1024)
+
+        idx = tile("idx", [P, S // 16], U16)
+        idx2 = tile("idx2", [P, PICKS // 16], U16)
+        near = tile("near", [P, PICKS // 16], U16)
+        tab = [tile("tab0", [P, T], I32), placed("tab1", [P, T], I32, 0)]
+        tab_sc = tile("tab_sc", [P, T], U8)
+        tab2 = placed("tab2", [P, T3], I32, 0)
+        tab2_sc = tile("tab2_sc", [P, T3], U8)
+        w2 = placed("w2", [P, 2, 2 * N], U8, 10)
+        w2_sc = tile("w2_sc", [P, 2, N], U8)
+        wb = placed("wb", [P, N], I32, 8)
+        wb_sc = tile("wb_sc", [P, N], U8)
+        rows_sb = tile("rows_sb", [P, K_PASS + P], F32)
+        ident = tile("ident", [P, P], F32)
+        b1_sb = tile("b1_sb", [P, PACK, 2], F32)
+        ba_sb = tile("ba_sb", [P, N // P], F32)
+        raw = tile("raw", [P, PACK, K_PASS], F32)
+        w1_raw = {(0, 0): raw, (1, 0): raw, (0, 1): raw, (1, 1): placed("raw11", [P, PACK, K_PASS], F32, 18)}
+        wa_raw = raw
+        w16 = {
+            (0, 0): placed("w16_00", [P, PACK * K_PASS], BF16, 14),
+            (1, 0): placed("w16_10", [P, PACK * K_PASS], BF16, 18),
+            (0, 1): tile("w16_01", [P, PACK * K_PASS], BF16),
+            (1, 1): tile("w16_11", [P, PACK * K_PASS], BF16),
+        }
+        wa16 = tile("wa16", [P, PACK * N], BF16)
+        w1_q = {(a, b): tile(f"w1_q{a}{b}", [P, K_PASS], U32) for a in range(2) for b in range(2)}
+        w1_sc = {(a, b): tile(f"w1_sc{a}{b}", [P, K_PASS], U8) for a in range(2) for b in range(2)}
+        wa_q = tile("wa_q", [P, N], U32)
+        wa_sc = tile("wa_sc", [P, N], U8)
+        v = {(a, j): tile(f"v{a}{j}", [P, BANK], U32) for a, j in ((0, 1), (1, 0), (1, 1))}
+        v[0, 0] = placed("v00", [P, BANK], U32, 16)
+        v_sc = tile("v_sc", [P, S], U8)
+        v2 = tile("v2", [P, PICKS], U32)
+        v2_sc = tile("v2_sc", [P, PICKS], U8)
+        th = [tile(f"th{i}", [P, PACK, BANK], F32) for i in range(4)]
+        h16 = [w16[1, 1], w16[0, 1]]
+        h_q = {(b, j): tile(f"h_q{b}{j}", [P, BANK], U32) for b in range(2) for j in range(2)}
+        h_sc = {(b, j): tile(f"h_sc{b}{j}", [P, BANK], U8) for b in range(2) for j in range(2)}
+        y = [tile(f"y{n}", [P, S], F32) for n in range(4)]
+        qb = [tile(f"qb{n}", [P, PICKS], F32) for n in range(4)]
+        top = [tile(f"top{n}", [P, PICKS], F32) for n in range(4)]
+        res = [tile(f"res{n}", [P, PICKS], F32) for n in range(4)]
+        first = [psum.tile([P, BANK], F32, name=f"first{t}") for t in range(4)]
+        spare = [psum.tile([P, BANK], F32, name=f"spare{n}") for n in range(3)]
+        vec = psum.tile([P, BANK], F32, name="vec")
+
+        nc.vector.memset(tab_sc[:].bitcast(I32), 0)
+        nc.vector.memset(rows_sb[:], 0.0)
+        for plane in (tab2_sc[:], wb_sc[:], w2_sc[:].rearrange("p a n -> p (a n)")):
+            nc.vector.memset(plane.bitcast(I32), 0)
+
+        def load_w1(a, b):
+            rows = w1[a * K_PASS : (a + 1) * K_PASS, b * K_PASS : (b + 1) * K_PASS]
+            nc.sync.dma_start(out=w1_raw[a, b][:], in_=rows.rearrange("(p i) c -> p i c", i=PACK))
+
+        def load_tab(a):
+            nc.sync.dma_start(out=tab[a][:], in_=tab_words[a].rearrange("p t i -> p (t i)").bitcast(I32))
+
+        load_w1(0, 0)
+        load_tab(0)
+        nc.sync.dma_start(idx[:], offs)
+        nc.sync.dma_start(idx2[:], offs2)
+        nc.sync.dma_start(near[:], pos1)
+        nc.sync.dma_start(out=rows_sb[0:2, 0:K_PASS], in_=b1.rearrange("(b c) -> b c", b=2))
+        nc.sync.dma_start(out=rows_sb[2:4, 0:K_PASS], in_=gain.rearrange("(b c) -> b c", b=2))
+        nc.sync.dma_start(out=rows_sb[0:4, K_PASS:], in_=ba.rearrange("(n p) -> n p", p=P))
+        for q in range(QUADS):
+            nc.gpsimd.dma_start(
+                out=tab_sc[32 * q : 32 * q + 8, :].bitcast(I32),
+                in_=tab_scales[:, 4 * q : 4 * q + 4, :].bitcast(I32),
+            )
+        make_identity(nc, ident[:])
+        for q in range(QUADS):
+            nc.gpsimd.dma_start(
+                out=tab2_sc[32 * q : 32 * q + 4, :].bitcast(I32),
+                in_=tab2_scales[0, 4 * q : 4 * q + 4, :].bitcast(I32),
+            )
+        for q in range(QUADS):
+            nc.gpsimd.dma_start(
+                out=wb_sc[32 * q : 32 * q + 4, :].bitcast(I32),
+                in_=wb_scales[0, 4 * q : 4 * q + 4, :].bitcast(I32),
+            )
+        for q in range(QUADS):
+            nc.gpsimd.dma_start(
+                out=w2_sc[32 * q : 32 * q + 4, :, :].bitcast(I32),
+                in_=w2_scales[:, 4 * q : 4 * q + 4, :].rearrange("a r c -> r a c").bitcast(I32),
+            )
+
+        by_t = vec[:].rearrange("p (t r) -> p t r", t=PACK)
+        for t in range(PACK):
+            nc.tensor.transpose(by_t[:, t, :], rows_sb[:, t:K_PASS:PACK], ident[:])
+        nc.tensor.transpose(spare[0][:, 0:P], rows_sb[:, K_PASS:], ident[:])
+        nc.scalar.copy(out=b1_sb[:], in_=by_t[:, :, 0:2])
+        nc.scalar.copy(out=ba_sb[:], in_=spare[0][:, 0 : N // P])
+
+        def copy_on(engine, dst, src):
+            if engine == "scalar":
+                nc.scalar.copy(out=dst, in_=src)
+            else:
+                nc.vector.tensor_copy(out=dst, in_=src)
+
+        def round_w1(a, b, engine):
+            copy_on(
+                engine,
+                w16[a, b][:].rearrange("p (t m i) -> p m i t", t=PACK, i=PACK),
+                w1_raw[a, b][:].rearrange("p i (m t) -> p m i t", t=PACK),
+            )
+
+        def quantize(codes, scales, stage):
+            nc.vector.quantize_mx(out=codes[:].bitcast(FP8X4), scales=scales[:], in_=stage[:])
+
+        def gather_v(a, j):
+            nc.vector.tensor_copy(v[a, j][:], tab[a][:].bitcast(U32).indirect(idx[:, 32 * j : 32 * (j + 1)]))
+
+        def first_pass(a, b, j):
+            for t in range(PACK):
+                cols = slice(t * P, (t + 1) * P)
+                nc.tensor.matmul_mx(
+                    out=first[t][:],
+                    lhsT=w1_q[a, b][:, cols].bitcast(FP8X4),
+                    lhsT_scale=w1_sc[a, b][:, cols],
+                    rhs=v[a, j][:].bitcast(FP8X4),
+                    rhs_scale=v_sc[4 * a : P, j * BANK : (j + 1) * BANK],
+                    start=(a == 0),
+                    stop=(a == 1),
+                )
+
+        def tanh(b, stage):
+            for t in range(PACK):
+                nc.scalar.activation(out=stage[:, t, :], in_=first[t][:], func=ACT.Tanh, bias=b1_sb[:, t, b : b + 1])
+
+        def apply_gain(b, src, stage):
+            nc.vector.tensor_tensor(
+                out=stage[:].rearrange("p (c i t) -> p c t i", i=4, t=PACK),
+                in0=src[:].rearrange("p t (c i) -> p c t i", i=4),
+                in1=by_t[:, :, 2 + b : 3 + b].unsqueeze(1).to_broadcast([P, BANK // 4, PACK, 4]),
+                op=ALU.mult,
+            )
+
+        def second_pass(b, j):
+            for n in range(4):
+                nc.tensor.matmul_mx(
+                    out=first[n][:],
+                    lhsT=w2[:, b, 2 * P * n : 2 * P * (n + 1)].bitcast(FP4X4),
+                    lhsT_scale=w2_sc[:, b, P * n : P * (n + 1)],
+                    rhs=h_q[b, j][:].bitcast(FP8X4),
+                    rhs_scale=h_sc[b, j][:],
+                    start=(b == 0),
+                    stop=(b == 1),
+                )
+
+        def keep_y(j):
+            for n in range(4):
+                nc.scalar.copy(out=y[n][:, j * BANK : (j + 1) * BANK], in_=first[n][:])
+
+        def question_pass(banks, codes, scales, tiles):
+            for n in tiles:
+                cols = slice(n * P, (n + 1) * P)
+                nc.tensor.matmul_mx(
+                    out=banks[n][:],
+                    lhsT=codes[:, cols].bitcast(FP8X4),
+                    lhsT_scale=scales[:, cols],
+                    rhs=v2[:].bitcast(FP8X4),
+                    rhs_scale=v2_sc[:],
+                    start=True,
+                    stop=True,
+                )
+
+        def quantize_w1(a, b):
+            quantize(w1_q[a, b], w1_sc[a, b], w16[a, b])
+
+        round_w1(0, 0, "scalar")
+        load_w1(1, 0)
+        quantize_w1(0, 0)
+        load_tab(1)
+        gather_v(0, 0)
+        gather_v(0, 1)
+        nc.vector.tensor_copy(v_sc[:], tab_sc[:].indirect(idx[:]))
+        round_w1(1, 0, "scalar")
+        load_w1(0, 1)
+        quantize_w1(1, 0)
+        load_w1(1, 1)
+        nc.vector.tensor_copy(v2_sc[:], tab2_sc[:].indirect(idx2[:]))
+        first_pass(0, 0, 0)
+        gather_v(1, 0)
+        first_pass(1, 0, 0)
+        tanh(0, th[0])
+        gather_v(1, 1)
+        nc.sync.dma_start(out=tab2[:], in_=tab2_words[0].rearrange("p t i -> p (t i)").bitcast(I32))
+        nc.sync.dma_start(out=wb[:], in_=wb_words[0].rearrange("p c i -> p (c i)").bitcast(I32))
+        nc.sync.dma_start(out=w2[:].bitcast(I32), in_=w2_words.rearrange("a p c -> p a c").bitcast(I32))
+        first_pass(0, 0, 1)
+        first_pass(1, 0, 1)
+        tanh(0, th[1])
+        round_w1(0, 1, "vector")
+        nc.sync.dma_start(out=wa_raw[:], in_=wa.rearrange("(p i) c -> p i c", i=PACK))
+        quantize_w1(0, 1)
+        round_w1(1, 1, "vector")
+        quantize_w1(1, 1)
+        first_pass(0, 1, 0)
+        first_pass(1, 1, 0)
+        tanh(1, th[2])
+        first_pass(0, 1, 1)
+        first_pass(1, 1, 1)
+        tanh(1, th[3])
+        apply_gain(0, th[0], h16[0])
+        apply_gain(0, th[1], h16[1])
+        quantize(h_q[0, 0], h_sc[0, 0], h16[0])
+        nc.vector.tensor_copy(v2[:], tab2[:].bitcast(U32).indirect(idx2[:]))
+        quantize(h_q[0, 1], h_sc[0, 1], h16[1])
+        nc.scalar.copy(
+            out=wa16[:].rearrange("p (c j i) -> p c i j", j=4, i=PACK),
+            in_=wa_raw[:].rearrange("p i (c j) -> p c i j", j=4),
+        )
+        qb_banks = spare + [spare[0]]
+        for n in range(4):
+            question_pass(qb_banks, wb[:].bitcast(U32), wb_sc[:], [n])
+            nc.scalar.copy(out=qb[n][:], in_=qb_banks[n][:])
+        apply_gain(1, th[2], h16[0])
+        quantize(h_q[1, 0], h_sc[1, 0], h16[0])
+        second_pass(0, 0)
+        second_pass(1, 0)
+        keep_y(0)
+        apply_gain(1, th[3], h16[1])
+        quantize(wa_q, wa_sc, wa16)
+        qa_banks = spare + [vec]
+        question_pass(qa_banks, wa_q[:], wa_sc[:], range(4))
+        second_pass(0, 1)
+        quantize(h_q[1, 1], h_sc[1, 1], h16[1])
+        second_pass(1, 1)
+        keep_y(1)
+        for n in range(4):
+            nc.vector.scalar_tensor_tensor(
+                out=top[n][:], in0=qa_banks[n][:], scalar=ba_sb[:, n : n + 1], in1=qb[n][:], op0=ALU.add, op1=ALU.max
+            )
+        for n in range(4):
+            nc.vector.tensor_tensor(res[n][:], y[n][:].indirect(near[:]), top[n][:], ALU.add)
+            nc.sync.dma_start(out=out[n * P : (n + 1) * P, :], in_=res[n][:])

@@ -22,6 +22,7 @@ PACK = 4
 K_PASS = P * PACK
 BANK = 512
 QUADS = 4
+VECTOR_COLS = 384
 
 
 def tile_list_inhaler_technique_grading_kernel(
@@ -43,53 +44,59 @@ def tile_list_inhaler_technique_grading_kernel(
         idx = tile("idx", [P, S // 16], U16)
         idx2 = tile("idx2", [P, PICKS // 16], U16)
         near = tile("near", [P, PICKS // 16], U16)
-        tab = [tile("tab0", [P, T], I32), placed("tab1", [P, T], I32, 0)]
-        tab_sc = tile("tab_sc", [P, T], U8)
-        tab2 = placed("tab2", [P, T3], I32, 0)
+        tab = [placed("tab0", [P, T], I32, 34), placed("tab1", [P, T], I32, 4)]
+        tab_sc = placed("tab_sc", [P, T], U8, 82)
+        tab2 = placed("tab2", [P, T3], I32, 4)
         tab2_sc = tile("tab2_sc", [P, T3], U8)
-        w2 = placed("w2", [P, 2, 2 * N], U8, 10)
-        w2_sc = tile("w2_sc", [P, 2, N], U8)
-        wb = placed("wb", [P, N], I32, 8)
-        wb_sc = tile("wb_sc", [P, N], U8)
+        wb = placed("wb", [P, N], I32, 36)
+        w2 = placed("w2", [P, 2, 2 * N], U8, 38)
+        wa_raw = placed("wa_raw", [P, PACK, N], F32, 28)
+        late_sc = placed("late_sc", [P, 3, N], U8, 42)
         rows_sb = tile("rows_sb", [P, K_PASS + P], F32)
         ident = tile("ident", [P, P], F32)
-        b1_sb = tile("b1_sb", [P, PACK, 2], F32)
+        vec_sb = tile("vec_sb", [P, PACK, 4], F32)
         ba_sb = tile("ba_sb", [P, N // P], F32)
-        raw = tile("raw", [P, PACK, K_PASS], F32)
-        w1_raw = {(0, 0): raw, (1, 0): raw, (0, 1): raw, (1, 1): placed("raw11", [P, PACK, K_PASS], F32, 18)}
-        wa_raw = raw
-        w16 = {
-            (0, 0): placed("w16_00", [P, PACK * K_PASS], BF16, 14),
-            (1, 0): placed("w16_10", [P, PACK * K_PASS], BF16, 18),
-            (0, 1): tile("w16_01", [P, PACK * K_PASS], BF16),
-            (1, 1): tile("w16_11", [P, PACK * K_PASS], BF16),
+        w1_raw = {
+            (0, 0): placed("raw00", [P, PACK, K_PASS], F32, 26),
+            (1, 0): placed("raw10", [P, PACK, K_PASS], F32, 26),
+            (0, 1): placed("raw01", [P, PACK, K_PASS], F32, 34),
+            (1, 1): placed("raw11", [P, PACK, K_PASS], F32, 42),
         }
-        wa16 = tile("wa16", [P, PACK * N], BF16)
+        stage = placed("stage", [P, PACK * K_PASS], BF16, 14)
+        w16 = {
+            (0, 0): placed("w16_00", [P, PACK * K_PASS], BF16, 2),
+            (1, 0): tile("w16_10", [P, PACK * K_PASS], BF16),
+            (0, 1): stage,
+            (1, 1): stage,
+        }
+        h16 = [placed("h16_0", [P, PACK * BANK], BF16, 12), placed("h16_1", [P, PACK * BANK], BF16, 16)]
         w1_q = {(a, b): tile(f"w1_q{a}{b}", [P, K_PASS], U32) for a in range(2) for b in range(2)}
         w1_sc = {(a, b): tile(f"w1_sc{a}{b}", [P, K_PASS], U8) for a in range(2) for b in range(2)}
         wa_q = tile("wa_q", [P, N], U32)
         wa_sc = tile("wa_sc", [P, N], U8)
-        v = {(a, j): tile(f"v{a}{j}", [P, BANK], U32) for a, j in ((0, 1), (1, 0), (1, 1))}
-        v[0, 0] = placed("v00", [P, BANK], U32, 16)
+        v = {(a, j): tile(f"v{a}{j}", [P, BANK], U32) for a, j in ((0, 1), (1, 1))}
+        v[1, 0] = placed("v10", [P, BANK], U32, 82)
+        v[0, 0] = placed("v00", [P, BANK], U32, 2)
         v_sc = tile("v_sc", [P, S], U8)
         v2 = tile("v2", [P, PICKS], U32)
         v2_sc = tile("v2_sc", [P, PICKS], U8)
-        th = [tile(f"th{i}", [P, PACK, BANK], F32) for i in range(4)]
-        h16 = [w16[1, 1], w16[0, 1]]
+        th = [placed(f"th{i}", [P, PACK, BANK], F32, 50 + 8 * i) for i in range(4)]
+        wa16 = placed("wa16", [P, PACK * N], BF16, 58)
         h_q = {(b, j): tile(f"h_q{b}{j}", [P, BANK], U32) for b in range(2) for j in range(2)}
         h_sc = {(b, j): tile(f"h_sc{b}{j}", [P, BANK], U8) for b in range(2) for j in range(2)}
         y = [tile(f"y{n}", [P, S], F32) for n in range(4)]
         qb = [tile(f"qb{n}", [P, PICKS], F32) for n in range(4)]
         top = [tile(f"top{n}", [P, PICKS], F32) for n in range(4)]
         res = [tile(f"res{n}", [P, PICKS], F32) for n in range(4)]
-        first = [psum.tile([P, BANK], F32, name=f"first{t}") for t in range(4)]
-        spare = [psum.tile([P, BANK], F32, name=f"spare{n}") for n in range(3)]
+        ring = [psum.tile([P, BANK], F32, name=f"ring{i}") for i in range(7)]
         vec = psum.tile([P, BANK], F32, name="vec")
 
-        nc.vector.memset(tab_sc[:].bitcast(I32), 0)
-        nc.vector.memset(rows_sb[:], 0.0)
-        for plane in (tab2_sc[:], wb_sc[:], w2_sc[:].rearrange("p a n -> p (a n)")):
-            nc.vector.memset(plane.bitcast(I32), 0)
+        def first_bank(b, j, t):
+            return ring[(PACK * (2 * b + j) + t) % len(ring)]
+
+        qb_banks = ring[2:6]
+        y_banks = [ring[6], ring[0], ring[1], ring[2]]
+        qa_banks = [vec, ring[3], ring[4], ring[5]]
 
         def load_w1(a, b):
             rows = w1[a * K_PASS : (a + 1) * K_PASS, b * K_PASS : (b + 1) * K_PASS]
@@ -98,6 +105,88 @@ def tile_list_inhaler_technique_grading_kernel(
         def load_tab(a):
             nc.sync.dma_start(out=tab[a][:], in_=tab_words[a].rearrange("p t i -> p (t i)").bitcast(I32))
 
+        def round_w1(a, b, copy):
+            copy(
+                out=w16[a, b][:].rearrange("p (t m i) -> p m i t", t=PACK, i=PACK),
+                in_=w1_raw[a, b][:].rearrange("p i (m t) -> p m i t", t=PACK),
+            )
+
+        def quantize(codes, scales, src):
+            nc.vector.quantize_mx(out=codes[:].bitcast(FP8X4), scales=scales[:], in_=src[:])
+
+        def quantize_w1(a, b):
+            quantize(w1_q[a, b], w1_sc[a, b], w16[a, b])
+
+        def gather_v(a, j):
+            nc.vector.tensor_copy(v[a, j][:], tab[a][:].bitcast(U32).indirect(idx[:, 32 * j : 32 * (j + 1)]))
+
+        def first_pass(a, b, j):
+            for t in range(PACK):
+                cols = slice(t * P, (t + 1) * P)
+                nc.tensor.matmul_mx(
+                    out=first_bank(b, j, t)[:],
+                    lhsT=w1_q[a, b][:, cols].bitcast(FP8X4),
+                    lhsT_scale=w1_sc[a, b][:, cols],
+                    rhs=v[a, j][:].bitcast(FP8X4),
+                    rhs_scale=v_sc[4 * a : P, j * BANK : (j + 1) * BANK],
+                    start=(a == 0),
+                    stop=(a == 1),
+                )
+
+        def tanh(b, j):
+            for t in range(PACK):
+                nc.scalar.activation(
+                    out=th[2 * b + j][:, t, :], in_=first_bank(b, j, t)[:], func=ACT.Tanh, bias=vec_sb[:, t, b : b + 1]
+                )
+
+        by_t = vec[:].rearrange("p (t r) -> p t r", t=PACK)
+
+        def apply_gain(b, src, dst):
+            nc.vector.tensor_tensor(
+                out=dst[:, 0 : PACK * VECTOR_COLS].rearrange("p (c i t) -> p c t i", i=4, t=PACK),
+                in0=src[:, :, 0:VECTOR_COLS].rearrange("p t (c i) -> p c t i", i=4),
+                in1=by_t[:, :, 2 + b : 3 + b].unsqueeze(1).to_broadcast([P, VECTOR_COLS // 4, PACK, 4]),
+                op=ALU.mult,
+            )
+            nc.gpsimd.tensor_tensor(
+                out=dst[:, PACK * VECTOR_COLS :].rearrange("p (j t) -> p j t", t=PACK),
+                in0=src[:, :, VECTOR_COLS:].rearrange("p t j -> p j t"),
+                in1=vec_sb[:, :, 2 + b].unsqueeze(1).to_broadcast([P, BANK - VECTOR_COLS, PACK]),
+                op=ALU.mult,
+            )
+
+        def second_pass(b, j):
+            for n in range(4):
+                nc.tensor.matmul_mx(
+                    out=y_banks[n][:],
+                    lhsT=w2[:, b, 2 * P * n : 2 * P * (n + 1)].bitcast(FP4X4),
+                    lhsT_scale=late_sc[:, 1 + b, P * n : P * (n + 1)],
+                    rhs=h_q[b, j][:].bitcast(FP8X4),
+                    rhs_scale=h_sc[b, j][:],
+                    start=(b == 0),
+                    stop=(b == 1),
+                )
+
+        def keep_y(j):
+            for n in range(4):
+                nc.scalar.copy(out=y[n][:, j * BANK : (j + 1) * BANK], in_=y_banks[n][:])
+
+        def question_pass(bank, codes, scales, n):
+            cols = slice(n * P, (n + 1) * P)
+            nc.tensor.matmul_mx(
+                out=bank[:],
+                lhsT=codes[:, cols].bitcast(FP8X4),
+                lhsT_scale=scales[:, cols],
+                rhs=v2[:].bitcast(FP8X4),
+                rhs_scale=v2_sc[:],
+                start=True,
+                stop=True,
+            )
+
+        nc.vector.memset(tab_sc[:].bitcast(I32), 0)
+        nc.vector.memset(rows_sb[:], 0.0)
+        nc.vector.memset(tab2_sc[:].bitcast(I32), 0)
+        make_identity(nc, ident[:])
         load_w1(0, 0)
         load_tab(0)
         nc.sync.dma_start(idx[:], offs)
@@ -111,164 +200,83 @@ def tile_list_inhaler_technique_grading_kernel(
                 out=tab_sc[32 * q : 32 * q + 8, :].bitcast(I32),
                 in_=tab_scales[:, 4 * q : 4 * q + 4, :].bitcast(I32),
             )
-        make_identity(nc, ident[:])
         for q in range(QUADS):
             nc.gpsimd.dma_start(
                 out=tab2_sc[32 * q : 32 * q + 4, :].bitcast(I32),
                 in_=tab2_scales[0, 4 * q : 4 * q + 4, :].bitcast(I32),
             )
-        for q in range(QUADS):
-            nc.gpsimd.dma_start(
-                out=wb_sc[32 * q : 32 * q + 4, :].bitcast(I32),
-                in_=wb_scales[0, 4 * q : 4 * q + 4, :].bitcast(I32),
-            )
-        for q in range(QUADS):
-            nc.gpsimd.dma_start(
-                out=w2_sc[32 * q : 32 * q + 4, :, :].bitcast(I32),
-                in_=w2_scales[:, 4 * q : 4 * q + 4, :].rearrange("a r c -> r a c").bitcast(I32),
-            )
 
-        by_t = vec[:].rearrange("p (t r) -> p t r", t=PACK)
-        for t in range(PACK):
-            nc.tensor.transpose(by_t[:, t, :], rows_sb[:, t:K_PASS:PACK], ident[:])
-        nc.tensor.transpose(spare[0][:, 0:P], rows_sb[:, K_PASS:], ident[:])
-        nc.scalar.copy(out=b1_sb[:], in_=by_t[:, :, 0:2])
-        nc.scalar.copy(out=ba_sb[:], in_=spare[0][:, 0 : N // P])
-
-        def copy_on(engine, dst, src):
-            if engine == "scalar":
-                nc.scalar.copy(out=dst, in_=src)
-            else:
-                nc.vector.tensor_copy(out=dst, in_=src)
-
-        def round_w1(a, b, engine):
-            copy_on(
-                engine,
-                w16[a, b][:].rearrange("p (t m i) -> p m i t", t=PACK, i=PACK),
-                w1_raw[a, b][:].rearrange("p i (m t) -> p m i t", t=PACK),
-            )
-
-        def quantize(codes, scales, stage):
-            nc.vector.quantize_mx(out=codes[:].bitcast(FP8X4), scales=scales[:], in_=stage[:])
-
-        def gather_v(a, j):
-            nc.vector.tensor_copy(v[a, j][:], tab[a][:].bitcast(U32).indirect(idx[:, 32 * j : 32 * (j + 1)]))
-
-        def first_pass(a, b, j):
-            for t in range(PACK):
-                cols = slice(t * P, (t + 1) * P)
-                nc.tensor.matmul_mx(
-                    out=first[t][:],
-                    lhsT=w1_q[a, b][:, cols].bitcast(FP8X4),
-                    lhsT_scale=w1_sc[a, b][:, cols],
-                    rhs=v[a, j][:].bitcast(FP8X4),
-                    rhs_scale=v_sc[4 * a : P, j * BANK : (j + 1) * BANK],
-                    start=(a == 0),
-                    stop=(a == 1),
-                )
-
-        def tanh(b, stage):
-            for t in range(PACK):
-                nc.scalar.activation(out=stage[:, t, :], in_=first[t][:], func=ACT.Tanh, bias=b1_sb[:, t, b : b + 1])
-
-        def apply_gain(b, src, stage):
-            nc.vector.tensor_tensor(
-                out=stage[:].rearrange("p (c i t) -> p c t i", i=4, t=PACK),
-                in0=src[:].rearrange("p t (c i) -> p c t i", i=4),
-                in1=by_t[:, :, 2 + b : 3 + b].unsqueeze(1).to_broadcast([P, BANK // 4, PACK, 4]),
-                op=ALU.mult,
-            )
-
-        def second_pass(b, j):
-            for n in range(4):
-                nc.tensor.matmul_mx(
-                    out=first[n][:],
-                    lhsT=w2[:, b, 2 * P * n : 2 * P * (n + 1)].bitcast(FP4X4),
-                    lhsT_scale=w2_sc[:, b, P * n : P * (n + 1)],
-                    rhs=h_q[b, j][:].bitcast(FP8X4),
-                    rhs_scale=h_sc[b, j][:],
-                    start=(b == 0),
-                    stop=(b == 1),
-                )
-
-        def keep_y(j):
-            for n in range(4):
-                nc.scalar.copy(out=y[n][:, j * BANK : (j + 1) * BANK], in_=first[n][:])
-
-        def question_pass(banks, codes, scales, tiles):
-            for n in tiles:
-                cols = slice(n * P, (n + 1) * P)
-                nc.tensor.matmul_mx(
-                    out=banks[n][:],
-                    lhsT=codes[:, cols].bitcast(FP8X4),
-                    lhsT_scale=scales[:, cols],
-                    rhs=v2[:].bitcast(FP8X4),
-                    rhs_scale=v2_sc[:],
-                    start=True,
-                    stop=True,
-                )
-
-        def quantize_w1(a, b):
-            quantize(w1_q[a, b], w1_sc[a, b], w16[a, b])
-
-        round_w1(0, 0, "scalar")
+        round_w1(0, 0, nc.scalar.copy)
         load_w1(1, 0)
         quantize_w1(0, 0)
         load_tab(1)
         gather_v(0, 0)
         gather_v(0, 1)
-        nc.vector.tensor_copy(v_sc[:], tab_sc[:].indirect(idx[:]))
-        round_w1(1, 0, "scalar")
         load_w1(0, 1)
-        quantize_w1(1, 0)
         load_w1(1, 1)
+        nc.vector.tensor_copy(v_sc[:], tab_sc[:].indirect(idx[:]))
+        round_w1(1, 0, nc.scalar.copy)
+        quantize_w1(1, 0)
         nc.vector.tensor_copy(v2_sc[:], tab2_sc[:].indirect(idx2[:]))
+        for t in range(PACK):
+            nc.tensor.transpose(by_t[:, t, :], rows_sb[:, t:K_PASS:PACK], ident[:])
+        nc.tensor.transpose(ring[6][:, 0:P], rows_sb[:, K_PASS:], ident[:])
+        nc.scalar.copy(out=vec_sb[:], in_=by_t[:, :, 0:4])
+        nc.scalar.copy(out=ba_sb[:], in_=ring[6][:, 0 : N // P])
         first_pass(0, 0, 0)
-        gather_v(1, 0)
+        for j in range(2):
+            gather_v(1, j)
         first_pass(1, 0, 0)
-        tanh(0, th[0])
-        gather_v(1, 1)
-        nc.sync.dma_start(out=tab2[:], in_=tab2_words[0].rearrange("p t i -> p (t i)").bitcast(I32))
-        nc.sync.dma_start(out=wb[:], in_=wb_words[0].rearrange("p c i -> p (c i)").bitcast(I32))
-        nc.sync.dma_start(out=w2[:].bitcast(I32), in_=w2_words.rearrange("a p c -> p a c").bitcast(I32))
+        tanh(0, 0)
         first_pass(0, 0, 1)
         first_pass(1, 0, 1)
-        tanh(0, th[1])
-        round_w1(0, 1, "vector")
+        tanh(0, 1)
+        nc.sync.dma_start(out=tab2[:], in_=tab2_words[0].rearrange("p t i -> p (t i)").bitcast(I32))
+        round_w1(0, 1, nc.vector.tensor_copy)
+        nc.sync.dma_start(out=wb[:], in_=wb_words[0].rearrange("p c i -> p (c i)").bitcast(I32))
+        nc.sync.dma_start(out=w2[:].bitcast(I32), in_=w2_words.rearrange("a p c -> p a c").bitcast(I32))
         nc.sync.dma_start(out=wa_raw[:], in_=wa.rearrange("(p i) c -> p i c", i=PACK))
         quantize_w1(0, 1)
-        round_w1(1, 1, "vector")
+        round_w1(1, 1, nc.vector.tensor_copy)
+        nc.vector.memset(late_sc[:].rearrange("p a n -> p (a n)").bitcast(I32), 0)
         quantize_w1(1, 1)
-        first_pass(0, 1, 0)
-        first_pass(1, 1, 0)
-        tanh(1, th[2])
-        first_pass(0, 1, 1)
-        first_pass(1, 1, 1)
-        tanh(1, th[3])
+        for q in range(QUADS):
+            nc.sync.dma_start(
+                out=late_sc[32 * q : 32 * q + 4, 0, :].bitcast(I32),
+                in_=wb_scales[0, 4 * q : 4 * q + 4, :].bitcast(I32),
+            )
+        for q in range(QUADS):
+            nc.sync.dma_start(
+                out=late_sc[32 * q : 32 * q + 4, 1:3, :].bitcast(I32),
+                in_=w2_scales[:, 4 * q : 4 * q + 4, :].rearrange("a r c -> r a c").bitcast(I32),
+            )
+        for j in range(2):
+            first_pass(0, 1, j)
+            first_pass(1, 1, j)
+            tanh(1, j)
         apply_gain(0, th[0], h16[0])
         apply_gain(0, th[1], h16[1])
         quantize(h_q[0, 0], h_sc[0, 0], h16[0])
-        nc.vector.tensor_copy(v2[:], tab2[:].bitcast(U32).indirect(idx2[:]))
         quantize(h_q[0, 1], h_sc[0, 1], h16[1])
         nc.scalar.copy(
             out=wa16[:].rearrange("p (c j i) -> p c i j", j=4, i=PACK),
             in_=wa_raw[:].rearrange("p i (c j) -> p c i j", j=4),
         )
-        qb_banks = spare + [spare[0]]
+        apply_gain(1, th[2], h16[1])
+        nc.vector.tensor_copy(v2[:], tab2[:].bitcast(U32).indirect(idx2[:]))
+        quantize(h_q[1, 0], h_sc[1, 0], h16[1])
         for n in range(4):
-            question_pass(qb_banks, wb[:].bitcast(U32), wb_sc[:], [n])
+            question_pass(qb_banks[n], wb[:].bitcast(U32), late_sc[:, 0, :], n)
             nc.scalar.copy(out=qb[n][:], in_=qb_banks[n][:])
-        apply_gain(1, th[2], h16[0])
-        quantize(h_q[1, 0], h_sc[1, 0], h16[0])
         second_pass(0, 0)
         second_pass(1, 0)
         keep_y(0)
-        apply_gain(1, th[3], h16[1])
+        apply_gain(1, th[3], h16[0])
         quantize(wa_q, wa_sc, wa16)
-        qa_banks = spare + [vec]
-        question_pass(qa_banks, wa_q[:], wa_sc[:], range(4))
+        quantize(h_q[1, 1], h_sc[1, 1], h16[0])
+        for n in range(4):
+            question_pass(qa_banks[n], wa_q[:], wa_sc[:], n)
         second_pass(0, 1)
-        quantize(h_q[1, 1], h_sc[1, 1], h16[1])
         second_pass(1, 1)
         keep_y(1)
         for n in range(4):

@@ -79,7 +79,7 @@ def tile_list_inhaler_technique_grading_kernel(
         v[0, 0] = placed("v00", [P, BANK], U32, 2)
         v_sc = tile("v_sc", [P, S], U8)
         v2 = tile("v2", [P, PICKS], U32)
-        v2_sc = tile("v2_sc", [P, PICKS], U8)
+        v2_sc = placed("v2_sc", [P, PICKS], U8, 44)
         th = [placed(f"th{i}", [P, PACK, BANK], F32, 50 + 8 * i) for i in range(4)]
         wa16 = placed("wa16", [P, PACK * N], BF16, 58)
         h_q = {(b, j): tile(f"h_q{b}{j}", [P, BANK], U32) for b in range(2) for j in range(2)}
@@ -105,10 +105,10 @@ def tile_list_inhaler_technique_grading_kernel(
         def load_tab(a):
             nc.sync.dma_start(out=tab[a][:], in_=tab_words[a].rearrange("p t i -> p (t i)").bitcast(I32))
 
-        def round_w1(a, b, copy):
+        def round_w1(a, b, copy, m0=0, m1=P):
             copy(
-                out=w16[a, b][:].rearrange("p (t m i) -> p m i t", t=PACK, i=PACK),
-                in_=w1_raw[a, b][:].rearrange("p i (m t) -> p m i t", t=PACK),
+                out=w16[a, b][:].rearrange("p (t m i) -> p m i t", t=PACK, i=PACK)[:, m0:m1],
+                in_=w1_raw[a, b][:].rearrange("p i (m t) -> p m i t", t=PACK)[:, m0:m1],
             )
 
         def quantize(codes, scales, src):
@@ -206,7 +206,8 @@ def tile_list_inhaler_technique_grading_kernel(
                 in_=tab2_scales[0, 4 * q : 4 * q + 4, :].bitcast(I32),
             )
 
-        round_w1(0, 0, nc.scalar.copy)
+        round_w1(0, 0, nc.vector.tensor_copy, 0, 80)
+        round_w1(0, 0, nc.scalar.copy, 80, P)
         load_w1(1, 0)
         quantize_w1(0, 0)
         load_tab(1)
@@ -217,7 +218,6 @@ def tile_list_inhaler_technique_grading_kernel(
         nc.vector.tensor_copy(v_sc[:], tab_sc[:].indirect(idx[:]))
         round_w1(1, 0, nc.scalar.copy)
         quantize_w1(1, 0)
-        nc.vector.tensor_copy(v2_sc[:], tab2_sc[:].indirect(idx2[:]))
         for t in range(PACK):
             nc.tensor.transpose(by_t[:, t, :], rows_sb[:, t:K_PASS:PACK], ident[:])
         nc.tensor.transpose(ring[6][:, 0:P], rows_sb[:, K_PASS:], ident[:])
@@ -263,6 +263,7 @@ def tile_list_inhaler_technique_grading_kernel(
             in_=wa_raw[:].rearrange("p i (c j) -> p c i j", j=4),
         )
         apply_gain(1, th[2], h16[1])
+        nc.vector.tensor_copy(v2_sc[:], tab2_sc[:].indirect(idx2[:]))
         nc.vector.tensor_copy(v2[:], tab2[:].bitcast(U32).indirect(idx2[:]))
         quantize(h_q[1, 0], h_sc[1, 0], h16[1])
         for n in range(4):

@@ -21,8 +21,16 @@ P = 128
 PACK = 4
 K_PASS = P * PACK
 BANK = 512
+LINE = 4
 QUADS = 4
-VECTOR_COLS = 384
+QUAD = P // QUADS
+QUAD_ROWS = 4
+LIST_ROWS = 16
+ROW_TILES = N // P
+RING = 7
+
+GAIN_COLS_VECTOR = 416
+ROUND_GROUPS_VECTOR = 80
 
 
 def tile_list_inhaler_technique_grading_kernel(
@@ -31,104 +39,124 @@ def tile_list_inhaler_technique_grading_kernel(
 ):
     nc = tc.nc
     with ExitStack() as ctx:
-        sb = ctx.enter_context(tc.tile_pool(name="sb", bufs=1))
-        reuse = ctx.enter_context(tc.tile_pool(name="reuse", bufs=1))
+        held = ctx.enter_context(tc.tile_pool(name="held", bufs=1))
+        shared = ctx.enter_context(tc.tile_pool(name="shared", bufs=1))
         psum = ctx.enter_context(tc.psum_pool(name="psum", bufs=1))
 
         def tile(name, shape, dtype):
-            return sb.tile(shape, dtype, name=name, align_bytes=64)
+            return held.tile(shape, dtype, name=name, align_bytes=64)
 
-        def placed(name, shape, dtype, kib):
-            return reuse.tile(shape, dtype, name=name, align_bytes=64, offset=kib * 1024)
+        def tile_at(kib, name, shape, dtype):
+            return shared.tile(shape, dtype, name=name, align_bytes=64, offset=kib * 1024)
 
-        idx = tile("idx", [P, S // 16], U16)
-        idx2 = tile("idx2", [P, PICKS // 16], U16)
-        near = tile("near", [P, PICKS // 16], U16)
-        tab = [placed("tab0", [P, T], I32, 34), placed("tab1", [P, T], I32, 4)]
-        tab_sc = placed("tab_sc", [P, T], U8, 82)
-        tab2 = placed("tab2", [P, T3], I32, 4)
-        tab2_sc = tile("tab2_sc", [P, T3], U8)
-        wb = placed("wb", [P, N], I32, 36)
-        w2 = placed("w2", [P, 2, 2 * N], U8, 38)
-        wa_raw = placed("wa_raw", [P, PACK, N], F32, 28)
-        late_sc = placed("late_sc", [P, 3, N], U8, 42)
-        rows_sb = tile("rows_sb", [P, K_PASS + P], F32)
+        pieces = [(first, second) for first in range(2) for second in range(2)]
+
+        idx = tile("idx", [P, S // LIST_ROWS], U16)
+        idx2 = tile("idx2", [P, PICKS // LIST_ROWS], U16)
+        near = tile("near", [P, PICKS // LIST_ROWS], U16)
+
+        w16_first = tile_at(0, "w16_first", [P, PACK * K_PASS], BF16)
+        v_first = tile_at(0, "v_first", [P, BANK], U32)
+        tab_pass1 = tile_at(2, "tab_pass1", [P, T], I32)
+        tab2 = tile_at(2, "tab2", [P, T3], I32)
+        w16_late = tile_at(12, "w16_late", [P, PACK * K_PASS], BF16)
+        h16 = [
+            tile_at(10, "h16_0", [P, PACK * BANK], BF16),
+            tile_at(14, "h16_1", [P, PACK * BANK], BF16),
+            tile("h16_2", [P, PACK * BANK], BF16),
+            tile("h16_3", [P, PACK * BANK], BF16),
+        ]
+        tab_pass0 = tile_at(32, "tab_pass0", [P, T], I32)
+        w1_raw = {
+            (0, 0): tile_at(24, "w1_raw00", [P, PACK, K_PASS], F32),
+            (1, 0): tile_at(24, "w1_raw10", [P, PACK, K_PASS], F32),
+            (0, 1): tile_at(32, "w1_raw01", [P, PACK, K_PASS], F32),
+            (1, 1): tile_at(40, "w1_raw11", [P, PACK, K_PASS], F32),
+        }
+        wa_raw = tile_at(26, "wa_raw", [P, PACK, N], F32)
+        wb = tile_at(34, "wb", [P, N], I32)
+        w2 = tile_at(36, "w2", [P, 2, 2 * N], U8)
+        weight_planes = tile_at(38, "weight_planes", [P, 3, N], U8)
+        th = [tile_at(48 + 8 * piece, f"th{piece}", [P, PACK, BANK], F32) for piece in range(4)]
+        wa16 = tile_at(56, "wa16", [P, PACK * N], BF16)
+        h_words = {(b, j): tile_at(72 + 2 * (2 * b + j), f"h_words{b}{j}", [P, BANK], U32) for b, j in pieces}
+        tab_planes = tile_at(80, "tab_planes", [P, T], U8)
+        v_third = tile_at(80, "v_third", [P, BANK], U32)
+
+        tab = [tab_pass0, tab_pass1]
+        tab2_plane = tile("tab2_plane", [P, T3], U8)
+        vec_rows = tile("vec_rows", [P, K_PASS + P], F32)
         ident = tile("ident", [P, P], F32)
         vec_sb = tile("vec_sb", [P, PACK, 4], F32)
-        ba_sb = tile("ba_sb", [P, N // P], F32)
-        w1_raw = {
-            (0, 0): placed("raw00", [P, PACK, K_PASS], F32, 26),
-            (1, 0): placed("raw10", [P, PACK, K_PASS], F32, 26),
-            (0, 1): placed("raw01", [P, PACK, K_PASS], F32, 34),
-            (1, 1): placed("raw11", [P, PACK, K_PASS], F32, 42),
-        }
-        stage = placed("stage", [P, PACK * K_PASS], BF16, 14)
+        ba_sb = tile("ba_sb", [P, ROW_TILES], F32)
         w16 = {
-            (0, 0): placed("w16_00", [P, PACK * K_PASS], BF16, 2),
-            (1, 0): tile("w16_10", [P, PACK * K_PASS], BF16),
-            (0, 1): stage,
-            (1, 1): stage,
+            (0, 0): w16_first,
+            (1, 0): tile("w16_second", [P, PACK * K_PASS], BF16),
+            (0, 1): w16_late,
+            (1, 1): w16_late,
         }
-        h16 = [placed("h16_0", [P, PACK * BANK], BF16, 12), placed("h16_1", [P, PACK * BANK], BF16, 16)]
-        w1_q = {(a, b): tile(f"w1_q{a}{b}", [P, K_PASS], U32) for a in range(2) for b in range(2)}
-        w1_sc = {(a, b): tile(f"w1_sc{a}{b}", [P, K_PASS], U8) for a in range(2) for b in range(2)}
-        wa_q = tile("wa_q", [P, N], U32)
-        wa_sc = tile("wa_sc", [P, N], U8)
-        v = {(a, j): tile(f"v{a}{j}", [P, BANK], U32) for a, j in ((0, 1), (1, 1))}
-        v[1, 0] = placed("v10", [P, BANK], U32, 82)
-        v[0, 0] = placed("v00", [P, BANK], U32, 2)
-        v_sc = tile("v_sc", [P, S], U8)
-        v2 = tile("v2", [P, PICKS], U32)
-        v2_sc = placed("v2_sc", [P, PICKS], U8, 44)
-        th = [placed(f"th{i}", [P, PACK, BANK], F32, 50 + 8 * i) for i in range(4)]
-        wa16 = placed("wa16", [P, PACK * N], BF16, 58)
-        h_q = {(b, j): tile(f"h_q{b}{j}", [P, BANK], U32) for b in range(2) for j in range(2)}
-        h_sc = {(b, j): tile(f"h_sc{b}{j}", [P, BANK], U8) for b in range(2) for j in range(2)}
-        y = [tile(f"y{n}", [P, S], F32) for n in range(4)]
-        qb = [tile(f"qb{n}", [P, PICKS], F32) for n in range(4)]
-        top = [tile(f"top{n}", [P, PICKS], F32) for n in range(4)]
-        res = [tile(f"res{n}", [P, PICKS], F32) for n in range(4)]
-        ring = [psum.tile([P, BANK], F32, name=f"ring{i}") for i in range(7)]
-        vec = psum.tile([P, BANK], F32, name="vec")
+        w1_words = {(a, b): tile(f"w1_words{a}{b}", [P, K_PASS], U32) for a, b in pieces}
+        w1_plane = {(a, b): tile(f"w1_plane{a}{b}", [P, K_PASS], U8) for a, b in pieces}
+        wa_words = tile("wa_words", [P, N], U32)
+        wa_plane = tile("wa_plane", [P, N], U8)
+        v_words = {
+            (0, 0): v_first,
+            (0, 1): tile("v_second", [P, BANK], U32),
+            (1, 0): v_third,
+            (1, 1): tile("v_fourth", [P, BANK], U32),
+        }
+        v_planes = tile("v_planes", [P, S], U8)
+        v2_words = tile("v2_words", [P, PICKS], U32)
+        v2_plane = tile("v2_plane", [P, PICKS], U8)
+        h_plane = {(b, j): tile(f"h_plane{b}{j}", [P, BANK], U8) for b, j in pieces}
+        y = [tile(f"y{n}", [P, S], F32) for n in range(ROW_TILES)]
+        qb = [tile(f"qb{n}", [P, PICKS], F32) for n in range(ROW_TILES)]
+        top = [tile(f"top{n}", [P, PICKS], F32) for n in range(ROW_TILES)]
+        res = [tile(f"res{n}", [P, PICKS], F32) for n in range(ROW_TILES)]
+
+        ring = [psum.tile([P, BANK], F32, name=f"ring{i}") for i in range(RING)]
+        vec_bank = psum.tile([P, BANK], F32, name="vec_bank")
+        qb_banks = ring[2:6]
+        qa_banks = [vec_bank] + ring[3:6]
+        y_banks = [ring[6]] + ring[0:3]
+        ba_bank = ring[6]
+        vec_ps = vec_bank[:].rearrange("p (t c) -> p t c", t=PACK)
 
         def first_bank(b, j, t):
-            return ring[(PACK * (2 * b + j) + t) % len(ring)]
-
-        qb_banks = ring[2:6]
-        y_banks = [ring[6], ring[0], ring[1], ring[2]]
-        qa_banks = [vec, ring[3], ring[4], ring[5]]
+            return ring[(PACK * (2 * b + j) + t) % RING]
 
         def load_w1(a, b):
             rows = w1[a * K_PASS : (a + 1) * K_PASS, b * K_PASS : (b + 1) * K_PASS]
             nc.sync.dma_start(out=w1_raw[a, b][:], in_=rows.rearrange("(p i) c -> p i c", i=PACK))
 
-        def load_tab(a):
-            nc.sync.dma_start(out=tab[a][:], in_=tab_words[a].rearrange("p t i -> p (t i)").bitcast(I32))
+        def load_words(dst, words):
+            nc.sync.dma_start(out=dst[:], in_=words.rearrange("p c i -> p (c i)").bitcast(I32))
 
-        def round_w1(a, b, copy, m0=0, m1=P):
+        def round_w1(a, b, copy, groups):
             copy(
-                out=w16[a, b][:].rearrange("p (t m i) -> p m i t", t=PACK, i=PACK)[:, m0:m1],
-                in_=w1_raw[a, b][:].rearrange("p i (m t) -> p m i t", t=PACK)[:, m0:m1],
+                out=w16[a, b][:].rearrange("p (t m i) -> p m i t", t=PACK, i=PACK)[:, groups],
+                in_=w1_raw[a, b][:].rearrange("p i (m t) -> p m i t", t=PACK)[:, groups],
             )
 
-        def quantize(codes, scales, src):
-            nc.vector.quantize_mx(out=codes[:].bitcast(FP8X4), scales=scales[:], in_=src[:])
+        def quantize(words, plane, rounded):
+            nc.vector.quantize_mx(out=words[:].bitcast(FP8X4), scales=plane[:], in_=rounded[:])
 
         def quantize_w1(a, b):
-            quantize(w1_q[a, b], w1_sc[a, b], w16[a, b])
+            quantize(w1_words[a, b], w1_plane[a, b], w16[a, b])
 
         def gather_v(a, j):
-            nc.vector.tensor_copy(v[a, j][:], tab[a][:].bitcast(U32).indirect(idx[:, 32 * j : 32 * (j + 1)]))
+            entries = idx[:, j * BANK // LIST_ROWS : (j + 1) * BANK // LIST_ROWS]
+            nc.vector.tensor_copy(v_words[a, j][:], tab[a][:].bitcast(U32).indirect(entries))
 
         def first_pass(a, b, j):
             for t in range(PACK):
                 cols = slice(t * P, (t + 1) * P)
                 nc.tensor.matmul_mx(
                     out=first_bank(b, j, t)[:],
-                    lhsT=w1_q[a, b][:, cols].bitcast(FP8X4),
-                    lhsT_scale=w1_sc[a, b][:, cols],
-                    rhs=v[a, j][:].bitcast(FP8X4),
-                    rhs_scale=v_sc[4 * a : P, j * BANK : (j + 1) * BANK],
+                    lhsT=w1_words[a, b][:, cols].bitcast(FP8X4),
+                    lhsT_scale=w1_plane[a, b][:, cols],
+                    rhs=v_words[a, j][:].bitcast(FP8X4),
+                    rhs_scale=v_planes[QUAD_ROWS * a : P, j * BANK : (j + 1) * BANK],
                     start=(a == 0),
                     stop=(a == 1),
                 )
@@ -139,90 +167,91 @@ def tile_list_inhaler_technique_grading_kernel(
                     out=th[2 * b + j][:, t, :], in_=first_bank(b, j, t)[:], func=ACT.Tanh, bias=vec_sb[:, t, b : b + 1]
                 )
 
-        by_t = vec[:].rearrange("p (t r) -> p t r", t=PACK)
-
-        def apply_gain(b, src, dst):
+        def apply_gain(b, j):
+            src, dst, split = th[2 * b + j], h16[2 * b + j], GAIN_COLS_VECTOR
             nc.vector.tensor_tensor(
-                out=dst[:, 0 : PACK * VECTOR_COLS].rearrange("p (c i t) -> p c t i", i=4, t=PACK),
-                in0=src[:, :, 0:VECTOR_COLS].rearrange("p t (c i) -> p c t i", i=4),
-                in1=by_t[:, :, 2 + b : 3 + b].unsqueeze(1).to_broadcast([P, VECTOR_COLS // 4, PACK, 4]),
+                out=dst[:, 0 : PACK * split].rearrange("p (c i t) -> p c t i", i=LINE, t=PACK),
+                in0=src[:, :, 0:split].rearrange("p t (c i) -> p c t i", i=LINE),
+                in1=vec_ps[:, :, 2 + b : 3 + b].unsqueeze(1).to_broadcast([P, split // LINE, PACK, LINE]),
                 op=ALU.mult,
             )
             nc.gpsimd.tensor_tensor(
-                out=dst[:, PACK * VECTOR_COLS :].rearrange("p (j t) -> p j t", t=PACK),
-                in0=src[:, :, VECTOR_COLS:].rearrange("p t j -> p j t"),
-                in1=vec_sb[:, :, 2 + b].unsqueeze(1).to_broadcast([P, BANK - VECTOR_COLS, PACK]),
+                out=dst[:, PACK * split :].rearrange("p (c t) -> p c t", t=PACK),
+                in0=src[:, :, split:].rearrange("p t c -> p c t"),
+                in1=vec_sb[:, :, 2 + b].unsqueeze(1).to_broadcast([P, BANK - split, PACK]),
                 op=ALU.mult,
             )
 
-        def second_pass(b, j):
-            for n in range(4):
-                nc.tensor.matmul_mx(
-                    out=y_banks[n][:],
-                    lhsT=w2[:, b, 2 * P * n : 2 * P * (n + 1)].bitcast(FP4X4),
-                    lhsT_scale=late_sc[:, 1 + b, P * n : P * (n + 1)],
-                    rhs=h_q[b, j][:].bitcast(FP8X4),
-                    rhs_scale=h_sc[b, j][:],
-                    start=(b == 0),
-                    stop=(b == 1),
-                )
-
-        def keep_y(j):
-            for n in range(4):
-                nc.scalar.copy(out=y[n][:, j * BANK : (j + 1) * BANK], in_=y_banks[n][:])
-
-        def question_pass(bank, codes, scales, n):
+        def question_pass(bank, words, plane, n):
             cols = slice(n * P, (n + 1) * P)
             nc.tensor.matmul_mx(
                 out=bank[:],
-                lhsT=codes[:, cols].bitcast(FP8X4),
-                lhsT_scale=scales[:, cols],
-                rhs=v2[:].bitcast(FP8X4),
-                rhs_scale=v2_sc[:],
+                lhsT=words[:, cols].bitcast(FP8X4),
+                lhsT_scale=plane[:, cols],
+                rhs=v2_words[:].bitcast(FP8X4),
+                rhs_scale=v2_plane[:],
                 start=True,
                 stop=True,
             )
 
-        nc.vector.memset(tab_sc[:].bitcast(I32), 0)
-        nc.vector.memset(rows_sb[:], 0.0)
-        nc.vector.memset(tab2_sc[:].bitcast(I32), 0)
+        def scores(n, j):
+            bank = y_banks[(2 * n + j) % len(y_banks)]
+            for b in range(2):
+                nc.tensor.matmul_mx(
+                    out=bank[:],
+                    lhsT=w2[:, b, 2 * P * n : 2 * P * (n + 1)].bitcast(FP4X4),
+                    lhsT_scale=weight_planes[:, 1 + b, P * n : P * (n + 1)],
+                    rhs=h_words[b, j][:].bitcast(FP8X4),
+                    rhs_scale=h_plane[b, j][:],
+                    start=(b == 0),
+                    stop=(b == 1),
+                )
+            nc.scalar.copy(out=y[n][:, j * BANK : (j + 1) * BANK], in_=bank[:])
+
+        nc.vector.memset(tab_planes[:].bitcast(I32), 0)
+        nc.vector.memset(vec_rows[:], 0.0)
+        nc.vector.memset(tab2_plane[:].bitcast(I32), 0)
         make_identity(nc, ident[:])
+
         load_w1(0, 0)
-        load_tab(0)
+        load_words(tab[0], tab_words[0])
         nc.sync.dma_start(idx[:], offs)
         nc.sync.dma_start(idx2[:], offs2)
         nc.sync.dma_start(near[:], pos1)
-        nc.sync.dma_start(out=rows_sb[0:2, 0:K_PASS], in_=b1.rearrange("(b c) -> b c", b=2))
-        nc.sync.dma_start(out=rows_sb[2:4, 0:K_PASS], in_=gain.rearrange("(b c) -> b c", b=2))
-        nc.sync.dma_start(out=rows_sb[0:4, K_PASS:], in_=ba.rearrange("(n p) -> n p", p=P))
+        nc.sync.dma_start(out=vec_rows[0:2, 0:K_PASS], in_=b1.rearrange("(b c) -> b c", b=2))
+        nc.sync.dma_start(out=vec_rows[2:4, 0:K_PASS], in_=gain.rearrange("(b c) -> b c", b=2))
+        nc.sync.dma_start(out=vec_rows[0:ROW_TILES, K_PASS:], in_=ba.rearrange("(n p) -> n p", p=P))
         for q in range(QUADS):
             nc.gpsimd.dma_start(
-                out=tab_sc[32 * q : 32 * q + 8, :].bitcast(I32),
-                in_=tab_scales[:, 4 * q : 4 * q + 4, :].bitcast(I32),
+                out=tab_planes[QUAD * q : QUAD * q + 2 * QUAD_ROWS, :].bitcast(I32),
+                in_=tab_scales[:, QUAD_ROWS * q : QUAD_ROWS * (q + 1), :].bitcast(I32),
             )
         for q in range(QUADS):
             nc.gpsimd.dma_start(
-                out=tab2_sc[32 * q : 32 * q + 4, :].bitcast(I32),
-                in_=tab2_scales[0, 4 * q : 4 * q + 4, :].bitcast(I32),
+                out=tab2_plane[QUAD * q : QUAD * q + QUAD_ROWS, :].bitcast(I32),
+                in_=tab2_scales[0, QUAD_ROWS * q : QUAD_ROWS * (q + 1), :].bitcast(I32),
             )
 
-        round_w1(0, 0, nc.vector.tensor_copy, 0, 80)
-        round_w1(0, 0, nc.scalar.copy, 80, P)
+        round_w1(0, 0, nc.vector.tensor_copy, slice(0, ROUND_GROUPS_VECTOR))
+        round_w1(0, 0, nc.scalar.copy, slice(ROUND_GROUPS_VECTOR, P))
         load_w1(1, 0)
         quantize_w1(0, 0)
-        load_tab(1)
-        gather_v(0, 0)
-        gather_v(0, 1)
+        load_words(tab[1], tab_words[1])
+        for j in range(2):
+            gather_v(0, j)
         load_w1(0, 1)
         load_w1(1, 1)
-        nc.vector.tensor_copy(v_sc[:], tab_sc[:].indirect(idx[:]))
-        round_w1(1, 0, nc.scalar.copy)
+        nc.vector.tensor_copy(v_planes[:], tab_planes[:].indirect(idx[:]))
+        round_w1(1, 0, nc.scalar.copy, slice(0, P))
         quantize_w1(1, 0)
+        nc.vector.tensor_copy(v2_plane[:], tab2_plane[:].indirect(idx2[:]))
+
         for t in range(PACK):
-            nc.tensor.transpose(by_t[:, t, :], rows_sb[:, t:K_PASS:PACK], ident[:])
-        nc.tensor.transpose(ring[6][:, 0:P], rows_sb[:, K_PASS:], ident[:])
-        nc.scalar.copy(out=vec_sb[:], in_=by_t[:, :, 0:4])
-        nc.scalar.copy(out=ba_sb[:], in_=ring[6][:, 0 : N // P])
+            nc.tensor.transpose(vec_ps[:, t, :], vec_rows[:, t:K_PASS:PACK], ident[:])
+        nc.tensor.transpose(ba_bank[:, 0:P], vec_rows[:, K_PASS:], ident[:])
+        nc.scalar.copy(out=vec_sb[:], in_=vec_ps[:, :, 0:4])
+        nc.scalar.copy(out=ba_sb[:], in_=ba_bank[:, 0:ROW_TILES])
+
         first_pass(0, 0, 0)
         for j in range(2):
             gather_v(1, j)
@@ -231,59 +260,59 @@ def tile_list_inhaler_technique_grading_kernel(
         first_pass(0, 0, 1)
         first_pass(1, 0, 1)
         tanh(0, 1)
-        nc.sync.dma_start(out=tab2[:], in_=tab2_words[0].rearrange("p t i -> p (t i)").bitcast(I32))
-        round_w1(0, 1, nc.vector.tensor_copy)
-        nc.sync.dma_start(out=wb[:], in_=wb_words[0].rearrange("p c i -> p (c i)").bitcast(I32))
-        nc.sync.dma_start(out=w2[:].bitcast(I32), in_=w2_words.rearrange("a p c -> p a c").bitcast(I32))
+
+        load_words(tab2, tab2_words[0])
+        round_w1(0, 1, nc.vector.tensor_copy, slice(0, P))
         nc.sync.dma_start(out=wa_raw[:], in_=wa.rearrange("(p i) c -> p i c", i=PACK))
+        load_words(wb, wb_words[0])
+        nc.sync.dma_start(out=w2[:].bitcast(I32), in_=w2_words.rearrange("a p c -> p a c").bitcast(I32))
+        nc.vector.memset(weight_planes[:].rearrange("p a n -> p (a n)").bitcast(I32), 0)
         quantize_w1(0, 1)
-        round_w1(1, 1, nc.vector.tensor_copy)
-        nc.vector.memset(late_sc[:].rearrange("p a n -> p (a n)").bitcast(I32), 0)
+        round_w1(1, 1, nc.vector.tensor_copy, slice(0, P))
         quantize_w1(1, 1)
         for q in range(QUADS):
             nc.sync.dma_start(
-                out=late_sc[32 * q : 32 * q + 4, 0, :].bitcast(I32),
-                in_=wb_scales[0, 4 * q : 4 * q + 4, :].bitcast(I32),
+                out=weight_planes[QUAD * q : QUAD * q + QUAD_ROWS, 0, :].bitcast(I32),
+                in_=wb_scales[0, QUAD_ROWS * q : QUAD_ROWS * (q + 1), :].bitcast(I32),
             )
         for q in range(QUADS):
             nc.sync.dma_start(
-                out=late_sc[32 * q : 32 * q + 4, 1:3, :].bitcast(I32),
-                in_=w2_scales[:, 4 * q : 4 * q + 4, :].rearrange("a r c -> r a c").bitcast(I32),
+                out=weight_planes[QUAD * q : QUAD * q + QUAD_ROWS, 1:3, :].bitcast(I32),
+                in_=w2_scales[:, QUAD_ROWS * q : QUAD_ROWS * (q + 1), :].rearrange("a r c -> r a c").bitcast(I32),
             )
         for j in range(2):
             first_pass(0, 1, j)
             first_pass(1, 1, j)
             tanh(1, j)
-        apply_gain(0, th[0], h16[0])
-        apply_gain(0, th[1], h16[1])
-        quantize(h_q[0, 0], h_sc[0, 0], h16[0])
-        quantize(h_q[0, 1], h_sc[0, 1], h16[1])
+
+        for j in range(2):
+            apply_gain(0, j)
+        nc.vector.tensor_copy(v2_words[:], tab2[:].bitcast(U32).indirect(idx2[:]))
+        for j in range(2):
+            apply_gain(1, j)
+
         nc.scalar.copy(
-            out=wa16[:].rearrange("p (c j i) -> p c i j", j=4, i=PACK),
-            in_=wa_raw[:].rearrange("p i (c j) -> p c i j", j=4),
+            out=wa16[:].rearrange("p (c e i) -> p c i e", e=LINE, i=PACK),
+            in_=wa_raw[:].rearrange("p i (c e) -> p c i e", e=LINE),
         )
-        apply_gain(1, th[2], h16[1])
-        nc.vector.tensor_copy(v2_sc[:], tab2_sc[:].indirect(idx2[:]))
-        nc.vector.tensor_copy(v2[:], tab2[:].bitcast(U32).indirect(idx2[:]))
-        quantize(h_q[1, 0], h_sc[1, 0], h16[1])
-        for n in range(4):
-            question_pass(qb_banks[n], wb[:].bitcast(U32), late_sc[:, 0, :], n)
+        for n in range(ROW_TILES):
+            question_pass(qb_banks[n], wb[:].bitcast(U32), weight_planes[:, 0, :], n)
             nc.scalar.copy(out=qb[n][:], in_=qb_banks[n][:])
-        second_pass(0, 0)
-        second_pass(1, 0)
-        keep_y(0)
-        apply_gain(1, th[3], h16[0])
-        quantize(wa_q, wa_sc, wa16)
-        quantize(h_q[1, 1], h_sc[1, 1], h16[0])
-        for n in range(4):
-            question_pass(qa_banks[n], wa_q[:], wa_sc[:], n)
-        second_pass(0, 1)
-        second_pass(1, 1)
-        keep_y(1)
-        for n in range(4):
+        quantize(wa_words, wa_plane, wa16)
+        for n in range(ROW_TILES):
+            question_pass(qa_banks[n], wa_words[:], wa_plane[:], n)
+
+        for j in range(2):
+            for b in range(2):
+                quantize(h_words[b, j], h_plane[b, j], h16[2 * b + j])
+        for n in range(ROW_TILES):
+            for j in range(2):
+                scores(n, j)
+
+        for n in range(ROW_TILES):
             nc.vector.scalar_tensor_tensor(
                 out=top[n][:], in0=qa_banks[n][:], scalar=ba_sb[:, n : n + 1], in1=qb[n][:], op0=ALU.add, op1=ALU.max
             )
-        for n in range(4):
+        for n in range(ROW_TILES):
             nc.vector.tensor_tensor(res[n][:], y[n][:].indirect(near[:]), top[n][:], ALU.add)
             nc.sync.dma_start(out=out[n * P : (n + 1) * P, :], in_=res[n][:])

from contextlib import ExitStack

import concourse.mybir as mybir
from concourse.masks import make_identity

K, H, N, K2, T, S, T3, PICKS = 1024, 1024, 512, 512, 4096, 1024, 2048, 512
FLOPS = 2 * K * H * S + 2 * H * N * S + 2 * 2 * K2 * N * PICKS

F32 = mybir.dt.float32
BF16 = mybir.dt.bfloat16
I32 = mybir.dt.int32
U32 = mybir.dt.uint32
U16 = mybir.dt.uint16
U8 = mybir.dt.uint8
FP8X4 = mybir.dt.float8_e4m3fn_x4
FP4X4 = mybir.dt.float4_e2m1fn_x4
ACT = mybir.ActivationFunctionType
ALU = mybir.AluOpType

P = 128
PACK = 4
K_PASS = P * PACK
BANK = 512
LINE = 4
QUADS = 4
QUAD = P // QUADS
QUAD_ROWS = 4
LIST_ROWS = 16
ROW_TILES = N // P
RING = 7

GAIN_COLS_VECTOR = 416
ROUND_GROUPS_VECTOR = 80


def tile_list_inhaler_technique_grading_kernel(
    tc, tab_words, tab_scales, tab2_words, tab2_scales, offs, offs2, pos1,
    w1, b1, gain, w2_words, w2_scales, wa, ba, wb_words, wb_scales, out,
):
    nc = tc.nc
    with ExitStack() as ctx:
        held = ctx.enter_context(tc.tile_pool(name="held", bufs=1))
        shared = ctx.enter_context(tc.tile_pool(name="shared", bufs=1))
        psum = ctx.enter_context(tc.psum_pool(name="psum", bufs=1))

        def tile(name, shape, dtype):
            return held.tile(shape, dtype, name=name, align_bytes=64)

        def tile_at(kib, name, shape, dtype):
            return shared.tile(shape, dtype, name=name, align_bytes=64, offset=kib * 1024)

        pieces = [(first, second) for first in range(2) for second in range(2)]

        idx = tile("idx", [P, S // LIST_ROWS], U16)
        idx2 = tile("idx2", [P, PICKS // LIST_ROWS], U16)
        near = tile("near", [P, PICKS // LIST_ROWS], U16)

        w16_first = tile_at(0, "w16_first", [P, PACK * K_PASS], BF16)
        v_first = tile_at(0, "v_first", [P, BANK], U32)
        tab_pass1 = tile_at(2, "tab_pass1", [P, T], I32)
        tab2 = tile_at(2, "tab2", [P, T3], I32)
        w16_late = tile_at(12, "w16_late", [P, PACK * K_PASS], BF16)
        h16 = [
            tile_at(10, "h16_0", [P, PACK * BANK], BF16),
            tile_at(14, "h16_1", [P, PACK * BANK], BF16),
            tile("h16_2", [P, PACK * BANK], BF16),
            tile("h16_3", [P, PACK * BANK], BF16),
        ]
        tab_pass0 = tile_at(32, "tab_pass0", [P, T], I32)
        w1_raw = {
            (0, 0): tile_at(24, "w1_raw00", [P, PACK, K_PASS], F32),
            (1, 0): tile_at(24, "w1_raw10", [P, PACK, K_PASS], F32),
            (0, 1): tile_at(32, "w1_raw01", [P, PACK, K_PASS], F32),
            (1, 1): tile_at(40, "w1_raw11", [P, PACK, K_PASS], F32),
        }
        wa_raw = tile_at(26, "wa_raw", [P, PACK, N], F32)
        wb = tile_at(34, "wb", [P, N], I32)
        w2 = tile_at(36, "w2", [P, 2, 2 * N], U8)
        weight_planes = tile_at(38, "weight_planes", [P, 3, N], U8)
        th = [tile_at(48 + 8 * piece, f"th{piece}", [P, PACK, BANK], F32) for piece in range(4)]
        wa16 = tile_at(56, "wa16", [P, PACK * N], BF16)
        h_words = {(b, j): tile_at(72 + 2 * (2 * b + j), f"h_words{b}{j}", [P, BANK], U32) for b, j in pieces}
        tab_planes = tile_at(80, "tab_planes", [P, T], U8)
        v_third = tile_at(80, "v_third", [P, BANK], U32)

        tab = [tab_pass0, tab_pass1]
        tab2_plane = tile("tab2_plane", [P, T3], U8)
        vec_rows = tile("vec_rows", [P, K_PASS + P], F32)
        ident = tile("ident", [P, P], F32)
        vec_sb = tile("vec_sb", [P, PACK, 4], F32)
        ba_sb = tile("ba_sb", [P, ROW_TILES], F32)
        w16 = {
            (0, 0): w16_first,
            (1, 0): tile("w16_second", [P, PACK * K_PASS], BF16),
            (0, 1): w16_late,
            (1, 1): w16_late,
        }
        w1_words = {(a, b): tile(f"w1_words{a}{b}", [P, K_PASS], U32) for a, b in pieces}
        w1_plane = {(a, b): tile(f"w1_plane{a}{b}", [P, K_PASS], U8) for a, b in pieces}
        wa_words = tile("wa_words", [P, N], U32)
        wa_plane = tile("wa_plane", [P, N], U8)
        v_words = {
            (0, 0): v_first,
            (0, 1): tile("v_second", [P, BANK], U32),
            (1, 0): v_third,
            (1, 1): tile("v_fourth", [P, BANK], U32),
        }
        v_planes = tile("v_planes", [P, S], U8)
        v2_words = tile("v2_words", [P, PICKS], U32)
        v2_plane = tile("v2_plane", [P, PICKS], U8)
        h_plane = {(b, j): tile(f"h_plane{b}{j}", [P, BANK], U8) for b, j in pieces}
        y = [tile(f"y{n}", [P, S], F32) for n in range(ROW_TILES)]
        qb = [tile(f"qb{n}", [P, PICKS], F32) for n in range(ROW_TILES)]
        top = [tile(f"top{n}", [P, PICKS], F32) for n in range(ROW_TILES)]
        res = [tile(f"res{n}", [P, PICKS], F32) for n in range(ROW_TILES)]

        ring = [psum.tile([P, BANK], F32, name=f"ring{i}") for i in range(RING)]
        vec_bank = psum.tile([P, BANK], F32, name="vec_bank")
        qb_banks = ring[2:6]
        qa_banks = [vec_bank] + ring[3:6]
        y_banks = [ring[6]] + ring[0:3]
        ba_bank = ring[6]
        vec_ps = vec_bank[:].rearrange("p (t c) -> p t c", t=PACK)

        def first_bank(b, j, t):
            return ring[(PACK * (2 * b + j) + t) % RING]

        def load_w1(a, b):
            rows = w1[a * K_PASS : (a + 1) * K_PASS, b * K_PASS : (b + 1) * K_PASS]
            nc.sync.dma_start(out=w1_raw[a, b][:], in_=rows.rearrange("(p i) c -> p i c", i=PACK))

        def load_words(dst, words):
            nc.sync.dma_start(out=dst[:], in_=words.rearrange("p c i -> p (c i)").bitcast(I32))

        def round_w1(a, b, copy, groups):
            copy(
                out=w16[a, b][:].rearrange("p (t m i) -> p m i t", t=PACK, i=PACK)[:, groups],
                in_=w1_raw[a, b][:].rearrange("p i (m t) -> p m i t", t=PACK)[:, groups],
            )

        def quantize(words, plane, rounded):
            nc.vector.quantize_mx(out=words[:].bitcast(FP8X4), scales=plane[:], in_=rounded[:])

        def quantize_w1(a, b):
            quantize(w1_words[a, b], w1_plane[a, b], w16[a, b])

        def gather_v(a, j):
            entries = idx[:, j * BANK // LIST_ROWS : (j + 1) * BANK // LIST_ROWS]
            nc.vector.tensor_copy(v_words[a, j][:], tab[a][:].bitcast(U32).indirect(entries))

        def first_pass(a, b, j):
            for t in range(PACK):
                cols = slice(t * P, (t + 1) * P)
                nc.tensor.matmul_mx(
                    out=first_bank(b, j, t)[:],
                    lhsT=w1_words[a, b][:, cols].bitcast(FP8X4),
                    lhsT_scale=w1_plane[a, b][:, cols],
                    rhs=v_words[a, j][:].bitcast(FP8X4),
                    rhs_scale=v_planes[QUAD_ROWS * a : P, j * BANK : (j + 1) * BANK],
                    start=(a == 0),
                    stop=(a == 1),
                )

        def tanh(b, j):
            for t in range(PACK):
                nc.scalar.activation(
                    out=th[2 * b + j][:, t, :], in_=first_bank(b, j, t)[:], func=ACT.Tanh, bias=vec_sb[:, t, b : b + 1]
                )

        def apply_gain(b, j):
            src, dst, split = th[2 * b + j], h16[2 * b + j], GAIN_COLS_VECTOR
            nc.vector.tensor_tensor(
                out=dst[:, 0 : PACK * split].rearrange("p (c i t) -> p c t i", i=LINE, t=PACK),
                in0=src[:, :, 0:split].rearrange("p t (c i) -> p c t i", i=LINE),
                in1=vec_ps[:, :, 2 + b : 3 + b].unsqueeze(1).to_broadcast([P, split // LINE, PACK, LINE]),
                op=ALU.mult,
            )
            nc.gpsimd.tensor_tensor(
                out=dst[:, PACK * split :].rearrange("p (c t) -> p c t", t=PACK),
                in0=src[:, :, split:].rearrange("p t c -> p c t"),
                in1=vec_sb[:, :, 2 + b].unsqueeze(1).to_broadcast([P, BANK - split, PACK]),
                op=ALU.mult,
            )

        def question_pass(bank, words, plane, n):
            cols = slice(n * P, (n + 1) * P)
            nc.tensor.matmul_mx(
                out=bank[:],
                lhsT=words[:, cols].bitcast(FP8X4),
                lhsT_scale=plane[:, cols],
                rhs=v2_words[:].bitcast(FP8X4),
                rhs_scale=v2_plane[:],
                start=True,
                stop=True,
            )

        def scores(n, j):
            bank = y_banks[(2 * n + j) % len(y_banks)]
            for b in range(2):
                nc.tensor.matmul_mx(
                    out=bank[:],
                    lhsT=w2[:, b, 2 * P * n : 2 * P * (n + 1)].bitcast(FP4X4),
                    lhsT_scale=weight_planes[:, 1 + b, P * n : P * (n + 1)],
                    rhs=h_words[b, j][:].bitcast(FP8X4),
                    rhs_scale=h_plane[b, j][:],
                    start=(b == 0),
                    stop=(b == 1),
                )
            nc.scalar.copy(out=y[n][:, j * BANK : (j + 1) * BANK], in_=bank[:])

        nc.vector.memset(tab_planes[:].bitcast(I32), 0)
        nc.vector.memset(vec_rows[:], 0.0)
        nc.vector.memset(tab2_plane[:].bitcast(I32), 0)
        make_identity(nc, ident[:])

        load_w1(0, 0)
        load_words(tab[0], tab_words[0])
        nc.sync.dma_start(idx[:], offs)
        nc.sync.dma_start(idx2[:], offs2)
        nc.sync.dma_start(near[:], pos1)
        nc.sync.dma_start(out=vec_rows[0:2, 0:K_PASS], in_=b1.rearrange("(b c) -> b c", b=2))
        nc.sync.dma_start(out=vec_rows[2:4, 0:K_PASS], in_=gain.rearrange("(b c) -> b c", b=2))
        nc.sync.dma_start(out=vec_rows[0:ROW_TILES, K_PASS:], in_=ba.rearrange("(n p) -> n p", p=P))
        for q in range(QUADS):
            nc.gpsimd.dma_start(
                out=tab_planes[QUAD * q : QUAD * q + 2 * QUAD_ROWS, :].bitcast(I32),
                in_=tab_scales[:, QUAD_ROWS * q : QUAD_ROWS * (q + 1), :].bitcast(I32),
            )
        for q in range(QUADS):
            nc.gpsimd.dma_start(
                out=tab2_plane[QUAD * q : QUAD * q + QUAD_ROWS, :].bitcast(I32),
                in_=tab2_scales[0, QUAD_ROWS * q : QUAD_ROWS * (q + 1), :].bitcast(I32),
            )

        round_w1(0, 0, nc.vector.tensor_copy, slice(0, ROUND_GROUPS_VECTOR))
        round_w1(0, 0, nc.scalar.copy, slice(ROUND_GROUPS_VECTOR, P))
        load_w1(1, 0)
        quantize_w1(0, 0)
        load_words(tab[1], tab_words[1])
        for j in range(2):
            gather_v(0, j)
        load_w1(0, 1)
        load_w1(1, 1)
        nc.vector.tensor_copy(v_planes[:], tab_planes[:].indirect(idx[:]))
        round_w1(1, 0, nc.scalar.copy, slice(0, P))
        quantize_w1(1, 0)
        nc.vector.tensor_copy(v2_plane[:], tab2_plane[:].indirect(idx2[:]))

        for t in range(PACK):
            nc.tensor.transpose(vec_ps[:, t, :], vec_rows[:, t:K_PASS:PACK], ident[:])
        nc.tensor.transpose(ba_bank[:, 0:P], vec_rows[:, K_PASS:], ident[:])
        nc.scalar.copy(out=vec_sb[:], in_=vec_ps[:, :, 0:4])
        nc.scalar.copy(out=ba_sb[:], in_=ba_bank[:, 0:ROW_TILES])

        first_pass(0, 0, 0)
        for j in range(2):
            gather_v(1, j)
        first_pass(1, 0, 0)
        tanh(0, 0)
        first_pass(0, 0, 1)
        first_pass(1, 0, 1)
        tanh(0, 1)

        load_words(tab2, tab2_words[0])
        round_w1(0, 1, nc.vector.tensor_copy, slice(0, P))
        nc.sync.dma_start(out=wa_raw[:], in_=wa.rearrange("(p i) c -> p i c", i=PACK))
        load_words(wb, wb_words[0])
        nc.sync.dma_start(out=w2[:].bitcast(I32), in_=w2_words.rearrange("a p c -> p a c").bitcast(I32))
        nc.vector.memset(weight_planes[:].rearrange("p a n -> p (a n)").bitcast(I32), 0)
        quantize_w1(0, 1)
        round_w1(1, 1, nc.vector.tensor_copy, slice(0, P))
        quantize_w1(1, 1)
        for q in range(QUADS):
            nc.sync.dma_start(
                out=weight_planes[QUAD * q : QUAD * q + QUAD_ROWS, 0, :].bitcast(I32),
                in_=wb_scales[0, QUAD_ROWS * q : QUAD_ROWS * (q + 1), :].bitcast(I32),
            )
        for q in range(QUADS):
            nc.sync.dma_start(
                out=weight_planes[QUAD * q : QUAD * q + QUAD_ROWS, 1:3, :].bitcast(I32),
                in_=w2_scales[:, QUAD_ROWS * q : QUAD_ROWS * (q + 1), :].rearrange("a r c -> r a c").bitcast(I32),
            )
        for j in range(2):
            first_pass(0, 1, j)
            first_pass(1, 1, j)
            tanh(1, j)

        for j in range(2):
            apply_gain(0, j)
        nc.vector.tensor_copy(v2_words[:], tab2[:].bitcast(U32).indirect(idx2[:]))
        for j in range(2):
            apply_gain(1, j)

        nc.scalar.copy(
            out=wa16[:].rearrange("p (c e i) -> p c i e", e=LINE, i=PACK),
            in_=wa_raw[:].rearrange("p i (c e) -> p c i e", e=LINE),
        )
        for n in range(ROW_TILES):
            question_pass(qb_banks[n], wb[:].bitcast(U32), weight_planes[:, 0, :], n)
            nc.scalar.copy(out=qb[n][:], in_=qb_banks[n][:])
        quantize(wa_words, wa_plane, wa16)
        for n in range(ROW_TILES):
            question_pass(qa_banks[n], wa_words[:], wa_plane[:], n)

        for j in range(2):
            for b in range(2):
                quantize(h_words[b, j], h_plane[b, j], h16[2 * b + j])
        for n in range(ROW_TILES):
            for j in range(2):
                scores(n, j)

        for n in range(ROW_TILES):
            nc.vector.scalar_tensor_tensor(
                out=top[n][:], in0=qa_banks[n][:], scalar=ba_sb[:, n : n + 1], in1=qb[n][:], op0=ALU.add, op1=ALU.max
            )
        for n in range(ROW_TILES):
            nc.vector.tensor_tensor(res[n][:], y[n][:].indirect(near[:]), top[n][:], ALU.add)
            nc.sync.dma_start(out=out[n * P : (n + 1) * P, :], in_=res[n][:])
